import numpy as np
import ml_dtypes


def mxq(x, axis, fmt="e4m3"):
    dtype, down = {"e4m3": (ml_dtypes.float8_e4m3fn, 7), "e5m2": (ml_dtypes.float8_e5m2, 14)}[fmt]
    v = np.moveaxis(np.asarray(x, np.float32).astype(ml_dtypes.bfloat16).astype(np.float64), axis, -1)
    blocks = v.reshape(v.shape[:-1] + (-1, 32))
    amax = np.abs(blocks).max(-1, keepdims=True)
    byte = np.maximum(np.where(amax > 0, np.frexp(amax)[1] - 1 + 127, 0) - down, 1)
    scale = np.exp2(byte - 127.0)
    codes = (blocks / scale).astype(np.float32).astype(dtype).astype(np.float64)
    return np.moveaxis((codes * scale).reshape(v.shape), -1, axis)


WIDE = False


def mx_kscale(k):
    if not WIDE:
        return np.ones(k)
    levels = np.array([10, -10, 5, -5, 0])
    if k % 512:
        return np.exp2(np.random.permutation(np.resize(levels, k // 32))).repeat(32)
    a = np.empty((k // 512, 16))
    for p in range(k // 512):
        a[p, :8] = np.random.permutation(np.resize(levels, 8))
        for g in range(8):
            far = levels[np.abs(levels - a[p, g]) >= 10]
            a[p, g + 8] = far[np.random.randint(len(far))]
    return np.exp2(a.ravel()).repeat(32)


BF16 = ml_dtypes.bfloat16


def bf(x):
    return np.asarray(x, np.float32).astype(BF16)


def f64(x):
    return np.asarray(x).astype(np.float64)


E2M1 = np.array([0.0, 0.5, 1.0, 1.5, 2.0, 3.0, 4.0, 6.0, -0.0, -0.5, -1.0, -1.5, -2.0, -3.0, -4.0, -6.0])


def pack_weight(w, fmt):
    k, n = w.shape
    w = f64(bf(w)).reshape(k // 32, 32, n)
    amax = np.abs(w).max(1)
    if fmt == "e4m3":
        byte = np.frexp(amax)[1] - 1 + 127 - 7
    else:
        mant, ex = np.frexp(amax / 6.0)
        byte = np.where(mant > 0.5, ex, ex - 1) + 127
    byte = np.clip(np.where(amax > 0, byte, 1), 1, 254)
    scaled = (w * np.exp2(127.0 - byte)[:, None, :]).reshape(k, n).astype(np.float32)
    by_word = np.ascontiguousarray(scaled.reshape(k // 512, 128, 4, n).transpose(0, 1, 3, 2))
    if fmt == "e4m3":
        words = by_word.astype(ml_dtypes.float8_e4m3fn).view(np.uint8)
    else:
        c = by_word.astype(ml_dtypes.float4_e2m1fn).view(np.uint8) & 0xF
        words = c[..., 0::2] | (c[..., 1::2] << 4)
    return np.ascontiguousarray(words), np.ascontiguousarray(byte.astype(np.uint8).reshape(k // 512, 16, n))


def unpack_weight(words, scales, fmt):
    g, p, n, _ = words.shape
    if fmt == "e4m3":
        vals = np.ascontiguousarray(words).view(ml_dtypes.float8_e4m3fn).astype(np.float64)
    else:
        nib = np.empty((g, p, n, 4), np.uint8)
        nib[..., 0::2] = words & 0xF
        nib[..., 1::2] = words >> 4
        vals = E2M1[nib]
    vals = vals * np.repeat(np.exp2(scales.astype(np.float64) - 127.0), 8, axis=1)[..., None]
    return vals.transpose(0, 1, 3, 2).reshape(g * 512, n)
def pack4(w):
    words, scales = pack_weight(w, "e2m1")
    return words.reshape(words.shape[0], 128, -1), scales


def unpack4(words, scales):
    return unpack_weight(words.reshape(words.shape[0], 128, -1, 2), scales, "e2m1")


M, KA, KB, R, N = 512, 512, 1024, 1536, 4096


def setup_inputs():
    sa, sb, tr = mx_kscale(KA), mx_kscale(KB), mx_kscale(R)
    inv_b = np.random.standard_normal((KB, R)) / np.sqrt(R) / sb[:, None]
    basis = np.random.standard_normal((R, N)) / np.sqrt(R) / tr[:, None]
    inv_b_words, inv_b_scales = pack4(inv_b)
    basis_words, basis_scales = pack4(basis)
    return {"vel_a": bf(1.5 * np.random.standard_normal((M, KA))),
            "grad_a": bf(np.random.standard_normal((M, KA)) * sa),
            "vel_b": bf(np.random.standard_normal((M, KB))),
            "grad_b": bf(np.random.standard_normal((M, KB)) * sb),
            "inv_a": bf(np.random.standard_normal((KA, R)) / np.sqrt(R) / sa[:, None]),
            "inv_b_words": inv_b_words, "inv_b_scales": inv_b_scales,
            "mean": bf(0.4 * np.random.standard_normal(R)),
            "filt": bf((1 + 0.1 * np.random.standard_normal(R)) * tr),
            "basis_words": basis_words, "basis_scales": basis_scales}


def reference(vel_a, grad_a, vel_b, grad_b, inv_a, inv_b_words, inv_b_scales, mean, filt, basis_words, basis_scales):
    fa = f64(vel_a) * f64(grad_a)
    fb = f64(vel_b) * f64(grad_b)
    inv_b = unpack4(inv_b_words, inv_b_scales)
    c = (mxq(fa, 1, "e4m3") @ mxq(f64(inv_a), 0, "e4m3")) + (mxq(fb, 1, "e4m3") @ inv_b)
    c = (c + f64(mean)) * f64(filt)
    basis = unpack4(basis_words, basis_scales)
    return mxq(c, 1, "e4m3") @ basis

@@ -1,0 +1,376 @@
+from contextlib import ExitStack
+
+import concourse.mybir as mybir
+from concourse.masks import make_identity
+
+M, KA, KB, R, N = 512, 512, 1024, 1536, 4096
+FLOPS = 2 * M * (KA + KB) * R + 2 * M * R * N
+
+F32 = mybir.dt.float32
+BF16 = mybir.dt.bfloat16
+I32 = mybir.dt.int32
+U32 = mybir.dt.uint32
+U8 = mybir.dt.uint8
+FP8X4 = mybir.dt.float8_e4m3fn_x4
+FP4X4 = mybir.dt.float4_e2m1fn_x4
+ADD = mybir.AluOpType.add
+MULT = mybir.AluOpType.mult
+
+P = 128
+W = 512
+BANKS = 8
+
+
+def tile_filtered_deim_advection_s3_kernel(
+    tc, vel_a, grad_a, vel_b, grad_b, inv_a, inv_b_words, inv_b_scales, mean, filt, basis_words, basis_scales, out
+):
+    nc = tc.nc
+    with ExitStack() as ctx:
+        sb = ctx.enter_context(tc.tile_pool(name="sb", bufs=1))
+        ps = ctx.enter_context(tc.psum_pool(name="ps", bufs=1))
+        ctx.enter_context(tc.manual_schedule())
+
+        taken = []
+
+        def next_bank():
+            k = len(taken)
+            bank = ps.tile([P, W], F32, name="bank%d" % k, tag="bank%d" % (k % BANKS))
+            taken.append(bank)
+            return bank
+
+        t = {}
+
+        def tile_rows(dram):
+            return dram.rearrange("(h p e) c -> h p e c", p=P, e=2)
+
+        def load_b(i):
+            for key, src in (("vel_b", vel_b), ("grad_b", grad_b)):
+                tile = sb.tile([P, KB], BF16, name="%s%d" % (key, i))
+                nc.sync.dma_start(out=tile[:], in_=tile_rows(src)[i // 2][:, i % 2, :])
+                t[key, i] = tile[:]
+
+        def load_a(h):
+            for key, src in (("vel_a", vel_a), ("grad_a", grad_a)):
+                tile = sb.tile([P, 2, KA], BF16, name="%s%d" % (key, h))
+                nc.sync.dma_start(out=tile[:], in_=tile_rows(src)[h])
+                for e in range(2):
+                    t[key, 2 * h + e] = tile[:, e, :]
+
+        def load_inv_a(j):
+            tile = sb.tile([P, 4, W], BF16, name="inv_a_raw%d" % j)
+            nc.sync.dma_start(out=tile[:], in_=inv_a[:, j * W : (j + 1) * W].rearrange("(p t) c -> p t c", t=4))
+            t["inv_a_raw", j] = tile
+
+        def load_words(key, src, j, cols):
+            groups = src.shape[0]
+            tile = sb.tile([P, groups, 2 * cols], U8, name="%s%d" % (key, j), align_bytes=64)
+            words = src.bitcast(I32).rearrange("g p w -> p g w")
+            nc.sync.dma_start(out=tile[:].bitcast(I32), in_=words[:, :, j * cols // 2 : (j + 1) * cols // 2])
+            t[key, j] = tile
+
+        def clear_plane(key, groups, j, cols):
+            tile = sb.tile([P, groups, cols], U8, name="%s%d" % (key, j), align_bytes=64)
+            nc.vector.memset(tile[:].bitcast(I32), 0)
+            t[key, j] = tile
+
+        def load_plane(key, src, j, cols):
+            rows = src.bitcast(I32).rearrange("g (q r) w -> r q g w", r=4)
+            for r in range(4):
+                nc.sync.dma_start(
+                    out=t[key, j][:].bitcast(I32)[r:P:32, :, :],
+                    in_=rows[r][:, :, j * cols // 4 : (j + 1) * cols // 4],
+                )
+
+        def load_vector(key, vec):
+            tile = sb.tile([P, 3, 4], BF16, name=key + "_col")
+            nc.scalar.dma_start(out=tile[:], in_=vec.rearrange("(g w t) -> w g t", g=3, t=4))
+            t[key, "col"] = tile
+
+        def spread_turn(j):
+            bank = next_bank()
+            for c, (key, u) in enumerate([("mean", 0), ("mean", 1), ("filt", 0), ("filt", 1)]):
+                col = t[key, "col"][:].bitcast(F32)[:, j, u : u + 1]
+                nc.tensor.transpose(bank[:, c * P : (c + 1) * P], col.to_broadcast([P, P]), ident[:])
+            t["spread_bank", j] = bank
+
+        def spread_copy(j, on_vector=False):
+            rows = sb.tile([P, W], F32, name="spread%d" % j)
+            if on_vector:
+                nc.vector.tensor_copy(out=rows[:], in_=t["spread_bank", j][:])
+            else:
+                nc.scalar.copy(out=rows[:], in_=t["spread_bank", j][:])
+            t["spread", j] = rows
+
+        def product(part, i):
+            vel, grad = t["vel_" + part, i], t["grad_" + part, i]
+            width = vel.shape[1]
+            tile = sb.tile([P, width], BF16, name="f%s%d" % (part, i), tag="f" + part, bufs=2)
+            nc.vector.tensor_tensor(
+                out=tile[:].rearrange("p (u w e) -> p u w e", u=2, e=2),
+                in0=vel.rearrange("p (w u e) -> p u w e", u=2, e=2),
+                in1=grad.rearrange("p (w u e) -> p u w e", u=2, e=2),
+                op=MULT,
+            )
+            words = tile[:].bitcast(F32)
+            half = width // 4
+            for g in range(width // W):
+                t["words", "f" + part, i, g] = [words[:, u * half + g * P : u * half + (g + 1) * P] for u in range(2)]
+
+        def turn(keys):
+            bank = next_bank()
+            for s, key in enumerate(keys):
+                for u in range(2):
+                    c = 2 * s + u
+                    nc.tensor.transpose(bank[:, c * P : (c + 1) * P], t[("words",) + key][u], ident[:])
+            t["turned", keys] = bank
+
+        def gather(keys):
+            n = len(keys)
+            tile = sb.tile([P, 2 * W], BF16, name="grouped_%s%d_%d" % keys[0], tag="grouped", bufs=4, align_bytes=64)
+            nc.scalar.copy(
+                out=tile[:, : n * W].bitcast(F32).rearrange("p (s m u) -> p s m u", s=n, u=2),
+                in_=t["turned", keys][:, : n * 2 * P].rearrange("p (s u m) -> p s m u", s=n, u=2),
+            )
+            t["grouped", keys] = tile
+
+        def quantise(keys):
+            n = len(keys)
+            codes = sb.tile([P, n * P], U32, name="codes_%s%d_%d" % keys[0], align_bytes=64)
+            scales = sb.tile([P, n * P], U8, name="scales_%s%d_%d" % keys[0], align_bytes=64)
+            nc.vector.quantize_mx(out=codes[:].bitcast(FP8X4), scales=scales[:], in_=t["grouped", keys][:, : n * W])
+            for s, key in enumerate(keys):
+                t[("lhs",) + key] = (codes[:, s * P : (s + 1) * P].bitcast(FP8X4), scales[:, s * P : (s + 1) * P])
+
+        def weave_inv_a(j, h, on_scalar):
+            tile = sb.tile([P, W // 2, 4], BF16, name="inv_a_woven%d_%d" % (j, h), align_bytes=64)
+            src = t["inv_a_raw", j][:, :, h * W // 2 : (h + 1) * W // 2].rearrange("p t c -> p c t")
+            if on_scalar:
+                nc.scalar.copy(out=tile[:], in_=src)
+            else:
+                nc.vector.tensor_copy(out=tile[:], in_=src)
+            t["inv_a_woven", j, h] = tile
+
+        def quantise_inv_a(j, h):
+            if h == 0:
+                t["inv_a_codes", j] = sb.tile([P, W], U32, name="inv_a_codes%d" % j, align_bytes=64)
+                t["inv_a_scales", j] = sb.tile([P, W], U8, name="inv_a_scales%d" % j, align_bytes=64)
+            cols = slice(h * W // 2, (h + 1) * W // 2)
+            nc.vector.quantize_mx(
+                out=t["inv_a_codes", j][:, cols].bitcast(FP8X4),
+                scales=t["inv_a_scales", j][:, cols],
+                in_=t["inv_a_woven", j, h][:].rearrange("p c t -> p (c t)"),
+            )
+
+        def passes(bank, pairs, first=True, last=True):
+            for s, (lhs, rhs) in enumerate(pairs):
+                nc.tensor.matmul_mx(
+                    out=bank[:], lhsT=lhs[0], lhsT_scale=lhs[1], rhs=rhs[0], rhs_scale=rhs[1],
+                    start=(first and s == 0), stop=(last and s == len(pairs) - 1),
+                )
+
+        def coeff_b(i, j):
+            bank = t["c_bank", i, j]
+            pairs = []
+            for g in range(2):
+                rhs = (t["inv_b", j][:, g, :].bitcast(FP4X4), t["inv_b_plane", 0][:, g, j * W : (j + 1) * W])
+                pairs.append((t["lhs", "fb", i, g], rhs))
+            passes(bank, pairs, first=False)
+
+        def coeff_a(i, j):
+            t["c_bank", i, j] = next_bank()
+            rhs = (t["inv_a_codes", j][:].bitcast(FP8X4), t["inv_a_scales", j][:])
+            passes(t["c_bank", i, j], [(t["lhs", "fa", i, 0], rhs)], last=False)
+
+        def coeff(i, j):
+            coeff_a(i, j)
+            coeff_b(i, j)
+
+        def offset(i, j):
+            tile = sb.tile([P, W], F32, name="shifted%d_%d" % (i, j), tag="shifted", bufs=3)
+            mean_rows = t["spread", j][:].bitcast(BF16)[:, :W]
+            nc.vector.tensor_tensor(
+                out=tile[:].rearrange("p (u w e) -> p u w e", u=2, e=2),
+                in0=t["c_bank", i, j][:].rearrange("p (w u e) -> p u w e", u=2, e=2),
+                in1=mean_rows.rearrange("p (u w e) -> p u w e", u=2, e=2),
+                op=ADD,
+            )
+            t["shifted", i, j] = tile
+
+        def damp(i, j):
+            tile = sb.tile([P, W], BF16, name="c%d_%d" % (i, j), tag="c", bufs=4)
+            filt_rows = t["spread", j][:].bitcast(BF16)[:, W:]
+            nc.vector.tensor_tensor(out=tile[:], in0=t["shifted", i, j][:], in1=filt_rows, op=MULT)
+            words = tile[:].bitcast(F32)
+            t["words", "c", i, j] = [words[:, u * P : (u + 1) * P] for u in range(2)]
+
+        def expand(i, n, on_vector=False, alone=False):
+            bank = next_bank()
+            pairs = []
+            for g in range(3):
+                words = t["basis", n // BQ][:, g, (n % BQ) * 2 * W : (n % BQ + 1) * 2 * W].bitcast(FP4X4)
+                plane = t["basis_plane", n // BH][:, g, (n % BH) * W : (n % BH + 1) * W]
+                pairs.append((t["lhs", "c", i, g], (words, plane)))
+            passes(bank, pairs)
+            if n % 2 == 0:
+                t["res", i, n // 2] = sb.tile([P, 2 * W], F32, name="res%d_%d" % (i, n // 2))
+            res = t["res", i, n // 2]
+            cols = slice((n % 2) * W, (n % 2 + 1) * W)
+            if on_vector:
+                nc.vector.tensor_copy(out=res[:, cols], in_=bank[:])
+            else:
+                nc.scalar.copy(out=res[:, cols], in_=bank[:])
+            rows = tile_rows(out)[i // 2][:, i % 2, :]
+            if alone:
+                nc.sync.dma_start(out=rows[:, n * W : (n + 1) * W], in_=res[:, cols])
+            elif n % 2 == 1:
+                nc.sync.dma_start(out=rows[:, (n - 1) * W : (n + 1) * W], in_=res[:])
+
+        ident = sb.tile([P, P], F32, name="ident")
+
+        def fb(i):
+            return (("fb", i, 0), ("fb", i, 1))
+
+        def fa(i):
+            return (("fa", i, 0),)
+
+        def c01(i):
+            return (("c", i, 0), ("c", i, 1))
+
+        def c2(i):
+            return (("c", i, 2),)
+
+        def filter_tile(i):
+            offset(i, 0)
+            offset(i, 1)
+            damp(i, 0)
+            offset(i, 2)
+            damp(i, 1)
+            damp(i, 2)
+
+        def turn_round(sets):
+            for s in sets:
+                turn(s)
+            for s in sets:
+                gather(s)
+                quantise(s)
+
+        def load_basis(q):
+            load_plane("basis_plane", basis_scales, q, BH * W)
+            load_words("basis", basis_words, q, BQ * W)
+
+        BQ, BH = 2, 2
+        load_vector("mean", mean)
+        load_vector("filt", filt)
+        make_identity(nc, ident[:])
+        clear_plane("inv_b_plane", 2, 0, R)
+        for q in range(4):
+            clear_plane("basis_plane", 3, q, BH * W)
+        load_inv_a(0)
+        load_b(0)
+        load_a(0)
+        load_inv_a(1)
+        load_inv_a(2)
+        load_plane("inv_b_plane", inv_b_scales, 0, R)
+        load_words("inv_b", inv_b_words, 0, W)
+        load_b(1)
+        load_words("inv_b", inv_b_words, 1, W)
+        load_words("inv_b", inv_b_words, 2, W)
+        load_basis(0)
+        load_basis(1)
+        load_b(2)
+        load_a(1)
+        load_basis(2)
+        load_basis(3)
+        load_b(3)
+
+        for j in range(3):
+            spread_turn(j)
+        spread_copy(0)
+        spread_copy(1, True)
+        weave_inv_a(0, 0, False)
+        weave_inv_a(0, 1, True)
+        product("b", 0)
+        quantise_inv_a(0, 0)
+        product("a", 0)
+        quantise_inv_a(0, 1)
+        product("a", 1)
+        turn(fb(0))
+        turn(fa(0) + fa(1))
+        spread_copy(2)
+        gather(fb(0))
+        gather(fa(0) + fa(1))
+        weave_inv_a(1, 0, False)
+        weave_inv_a(1, 1, True)
+        quantise(fb(0))
+        quantise(fa(0) + fa(1))
+        quantise_inv_a(1, 0)
+        coeff_a(0, 0)
+        weave_inv_a(2, 0, False)
+        weave_inv_a(2, 1, True)
+        quantise_inv_a(1, 1)
+        quantise_inv_a(2, 0)
+        coeff_a(1, 0)
+        coeff_b(0, 0)
+        coeff_a(0, 1)
+        quantise_inv_a(2, 1)
+        offset(0, 0)
+        product("b", 1)
+        coeff_a(0, 2)
+        coeff_b(0, 1)
+        turn(fb(1))
+        gather(fb(1))
+        damp(0, 0)
+        coeff_b(0, 2)
+        offset(0, 1)
+        quantise(fb(1))
+        offset(0, 2)
+        damp(0, 1)
+        damp(0, 2)
+        coeff_b(1, 0)
+        coeff(1, 1)
+        turn(c01(0))
+        gather(c01(0))
+        turn(c2(0))
+        gather(c2(0))
+        coeff(1, 2)
+        offset(1, 0)
+        quantise(c01(0))
+        quantise(c2(0))
+        offset(1, 1)
+        damp(1, 0)
+        offset(1, 2)
+        damp(1, 1)
+        damp(1, 2)
+        for n in range(3):
+            expand(0, n)
+        product("b", 2)
+        product("a", 2)
+        turn_round([c01(1), c2(1)])
+        product("a", 3)
+        expand(0, 3)
+        expand(1, 0)
+        turn_round([fb(2), fa(2) + fa(3)])
+        expand(1, 1)
+        expand(1, 2)
+        for j in range(3):
+            coeff(2, j)
+        filter_tile(2)
+        product("b", 3)
+        expand(1, 3)
+        for n in range(4, 8):
+            expand(0, n)
+        turn_round([c01(2), c2(2), fb(3)])
+        for n in range(4, 6):
+            expand(1, n)
+        for j in range(3):
+            coeff(3, j)
+        filter_tile(3)
+        for n in range(6, 8):
+            expand(1, n)
+        for n in range(0, 4):
+            expand(2, n)
+        turn_round([c01(3), c2(3)])
+        for n in range(4, 8):
+            expand(2, n)
+        for n in range(8):
+            expand(3, n, on_vector=(n % 2 == 1), alone=(n >= 6))

@@ -61,12 +61,13 @@ def tile_filtered_deim_advection_s3_kernel(
             nc.sync.dma_start(out=tile[:], in_=inv_a[:, j * W : (j + 1) * W].rearrange("(p t) c -> p t c", t=4))
             t["inv_a_raw", j] = tile
 
-        def load_words(key, src, j, cols):
+        def load_words(key, src, first, count):
             groups = src.shape[0]
-            tile = sb.tile([P, groups, 2 * cols], U8, name="%s%d" % (key, j), align_bytes=64)
+            tile = sb.tile([P, groups, 2 * W * count], U8, name="%s%d" % (key, first), align_bytes=64)
             words = src.bitcast(I32).rearrange("g p w -> p g w")
-            nc.sync.dma_start(out=tile[:].bitcast(I32), in_=words[:, :, j * cols // 2 : (j + 1) * cols // 2])
-            t[key, j] = tile
+            nc.sync.dma_start(out=tile[:].bitcast(I32), in_=words[:, :, first * W // 2 : (first + count) * W // 2])
+            for s in range(count):
+                t[key, first + s] = tile[:, :, s * 2 * W : (s + 1) * 2 * W]
 
         def clear_plane(key, groups, j, cols):
             tile = sb.tile([P, groups, cols], U8, name="%s%d" % (key, j), align_bytes=64)
@@ -143,11 +144,12 @@ def tile_filtered_deim_advection_s3_kernel(
 
         def weave_inv_a(j, h, on_scalar):
             tile = sb.tile([P, W // 2, 4], BF16, name="inv_a_woven%d_%d" % (j, h), align_bytes=64)
-            src = t["inv_a_raw", j][:, :, h * W // 2 : (h + 1) * W // 2].rearrange("p t c -> p c t")
+            src = t["inv_a_raw", j][:, :, h * W // 2 : (h + 1) * W // 2].rearrange("p t (c i) -> p c t i", i=4)
+            dst = tile[:].rearrange("p (c i) t -> p c t i", i=4)
             if on_scalar:
-                nc.scalar.copy(out=tile[:], in_=src)
+                nc.scalar.copy(out=dst, in_=src)
             else:
-                nc.vector.tensor_copy(out=tile[:], in_=src)
+                nc.vector.tensor_copy(out=dst, in_=src)
             t["inv_a_woven", j, h] = tile
 
         def quantise_inv_a(j, h):
@@ -207,7 +209,7 @@ def tile_filtered_deim_advection_s3_kernel(
             bank = next_bank()
             pairs = []
             for g in range(3):
-                words = t["basis", n // BQ][:, g, (n % BQ) * 2 * W : (n % BQ + 1) * 2 * W].bitcast(FP4X4)
+                words = t["basis", n][:, g, :].bitcast(FP4X4)
                 plane = t["basis_plane", n // BH][:, g, (n % BH) * W : (n % BH + 1) * W]
                 pairs.append((t["lhs", "c", i, g], (words, plane)))
             passes(bank, pairs)
@@ -258,29 +260,51 @@ def tile_filtered_deim_advection_s3_kernel(
             load_plane("basis_plane", basis_scales, q, BH * W)
             load_words("basis", basis_words, q, BQ * W)
 
-        BQ, BH = 2, 2
+        def expand_last(i, n):
+            rows = tile_rows(out)[i // 2][:, i % 2, :]
+            res = t["res", i, n // 2]
+            for s in range(4):
+                bank = next_bank()
+                pairs = []
+                for g in range(3):
+                    words = t["basis", n][:, g, s * 2 * P : (s + 1) * 2 * P].bitcast(FP4X4)
+                    plane = t["basis_plane", n // BH][:, g, (n % BH) * W + s * P : (n % BH) * W + (s + 1) * P]
+                    pairs.append((t["lhs", "c", i, g], (words, plane)))
+                passes(bank[:, :P], pairs)
+                cols = slice(W + s * P, W + (s + 1) * P)
+                if s % 2 == 1:
+                    nc.vector.tensor_copy(out=res[:, cols], in_=bank[:, :P])
+                    nc.sync.dma_start(out=rows[:, n * W + (s - 1) * P : n * W + (s + 1) * P], in_=res[:, W + (s - 1) * P : W + (s + 1) * P])
+                else:
+                    nc.scalar.copy(out=res[:, cols], in_=bank[:, :P])
+
+        def c1(i, j):
+            return (("c", i, j),)
+
+        BQ, BH = 2, 4
         load_vector("mean", mean)
         load_vector("filt", filt)
         make_identity(nc, ident[:])
         clear_plane("inv_b_plane", 2, 0, R)
-        for q in range(4):
+        for q in range(2):
             clear_plane("basis_plane", 3, q, BH * W)
         load_inv_a(0)
-        load_b(0)
         load_a(0)
+        load_b(0)
         load_inv_a(1)
         load_inv_a(2)
         load_plane("inv_b_plane", inv_b_scales, 0, R)
-        load_words("inv_b", inv_b_words, 0, W)
+        load_words("inv_b", inv_b_words, 0, 1)
         load_b(1)
-        load_words("inv_b", inv_b_words, 1, W)
-        load_words("inv_b", inv_b_words, 2, W)
-        load_basis(0)
-        load_basis(1)
+        load_words("inv_b", inv_b_words, 1, 2)
+        load_plane("basis_plane", basis_scales, 0, BH * W)
+        load_words("basis", basis_words, 0, 2)
+        load_words("basis", basis_words, 2, 2)
         load_b(2)
         load_a(1)
-        load_basis(2)
-        load_basis(3)
+        load_plane("basis_plane", basis_scales, 1, BH * W)
+        load_words("basis", basis_words, 4, 2)
+        load_words("basis", basis_words, 6, 2)
         load_b(3)
 
         for j in range(3):
@@ -289,48 +313,49 @@ def tile_filtered_deim_advection_s3_kernel(
         spread_copy(1, True)
         weave_inv_a(0, 0, False)
         weave_inv_a(0, 1, True)
-        product("b", 0)
-        quantise_inv_a(0, 0)
         product("a", 0)
-        quantise_inv_a(0, 1)
         product("a", 1)
-        turn(fb(0))
         turn(fa(0) + fa(1))
+        quantise_inv_a(0, 0)
+        quantise_inv_a(0, 1)
+        product("b", 0)
+        turn(fb(0))
         spread_copy(2)
-        gather(fb(0))
         gather(fa(0) + fa(1))
+        gather(fb(0))
+        quantise(fa(0) + fa(1))
+        coeff_a(0, 0)
+        coeff_a(1, 0)
         weave_inv_a(1, 0, False)
         weave_inv_a(1, 1, True)
         quantise(fb(0))
-        quantise(fa(0) + fa(1))
         quantise_inv_a(1, 0)
-        coeff_a(0, 0)
         weave_inv_a(2, 0, False)
         weave_inv_a(2, 1, True)
         quantise_inv_a(1, 1)
-        quantise_inv_a(2, 0)
-        coeff_a(1, 0)
-        coeff_b(0, 0)
         coeff_a(0, 1)
+        coeff_b(0, 0)
+        quantise_inv_a(2, 0)
         quantise_inv_a(2, 1)
-        offset(0, 0)
-        product("b", 1)
         coeff_a(0, 2)
-        coeff_b(0, 1)
+        coeff_a(1, 1)
+        product("b", 1)
+        offset(0, 0)
         turn(fb(1))
+        coeff_b(0, 1)
+        coeff_b(0, 2)
         gather(fb(1))
         damp(0, 0)
-        coeff_b(0, 2)
         offset(0, 1)
         quantise(fb(1))
+        coeff_b(1, 0)
+        coeff_b(1, 1)
         offset(0, 2)
         damp(0, 1)
         damp(0, 2)
-        coeff_b(1, 0)
-        coeff(1, 1)
         turn(c01(0))
-        gather(c01(0))
         turn(c2(0))
+        gather(c01(0))
         gather(c2(0))
         coeff(1, 2)
         offset(1, 0)
@@ -343,34 +368,36 @@ def tile_filtered_deim_advection_s3_kernel(
         damp(1, 2)
         for n in range(3):
             expand(0, n)
+        turn_round([c01(1), c2(1)])
         product("b", 2)
         product("a", 2)
-        turn_round([c01(1), c2(1)])
         product("a", 3)
         expand(0, 3)
-        expand(1, 0)
+        for n in range(0, 2):
+            expand(1, n)
         turn_round([fb(2), fa(2) + fa(3)])
-        expand(1, 1)
-        expand(1, 2)
+        for n in range(2, 4):
+            expand(1, n)
         for j in range(3):
             coeff(2, j)
         filter_tile(2)
         product("b", 3)
-        expand(1, 3)
-        for n in range(4, 8):
+        for n in range(4, 6):
+            expand(0, n)
+        for n in range(4, 6):
+            expand(1, n)
+        for n in range(6, 8):
             expand(0, n)
         turn_round([c01(2), c2(2), fb(3)])
-        for n in range(4, 6):
+        for n in range(6, 8):
             expand(1, n)
         for j in range(3):
             coeff(3, j)
         filter_tile(3)
-        for n in range(6, 8):
-            expand(1, n)
-        for n in range(0, 4):
+        for n in range(0, 6):
             expand(2, n)
         turn_round([c01(3), c2(3)])
-        for n in range(4, 8):
+        for n in range(6, 8):
             expand(2, n)
         for n in range(8):
-            expand(3, n, on_vector=(n % 2 == 1), alone=(n >= 6))
+            expand(3, n, on_vector=(n % 2 == 1), alone=(n >= 2))

@@ -74,10 +74,10 @@ def tile_filtered_deim_advection_s3_kernel(
             nc.vector.memset(tile[:].bitcast(I32), 0)
             t[key, j] = tile
 
-        def load_plane(key, src, j, cols):
+        def load_plane(key, src, j, cols, queue):
             rows = src.bitcast(I32).rearrange("g (q r) w -> r q g w", r=4)
             for r in range(4):
-                nc.sync.dma_start(
+                queue.dma_start(
                     out=t[key, j][:].bitcast(I32)[r:P:32, :, :],
                     in_=rows[r][:, :, j * cols // 4 : (j + 1) * cols // 4],
                 )
@@ -125,10 +125,11 @@ def tile_filtered_deim_advection_s3_kernel(
                     nc.tensor.transpose(bank[:, c * P : (c + 1) * P], t[("words",) + key][u], ident[:])
             t["turned", keys] = bank
 
-        def gather(keys):
+        def gather(keys, on_vector=False):
             n = len(keys)
+            move = nc.vector.tensor_copy if on_vector else nc.scalar.copy
             tile = sb.tile([P, 2 * W], BF16, name="grouped_%s%d_%d" % keys[0], tag="grouped", bufs=4, align_bytes=64)
-            nc.scalar.copy(
+            move(
                 out=tile[:, : n * W].bitcast(F32).rearrange("p (s m u) -> p s m u", s=n, u=2),
                 in_=t["turned", keys][:, : n * 2 * P].rearrange("p (s u m) -> p s m u", s=n, u=2),
             )
@@ -252,13 +253,12 @@ def tile_filtered_deim_advection_s3_kernel(
         def turn_round(sets):
             for s in sets:
                 turn(s)
-            for s in sets:
+            gather(sets[0], True)
+            for s in sets[1:]:
                 gather(s)
+            for s in sets:
                 quantise(s)
 
-        def load_basis(q):
-            load_plane("basis_plane", basis_scales, q, BH * W)
-            load_words("basis", basis_words, q, BQ * W)
 
         def expand_last(i, n):
             rows = tile_rows(out)[i // 2][:, i % 2, :]
@@ -281,30 +281,37 @@ def tile_filtered_deim_advection_s3_kernel(
         def c1(i, j):
             return (("c", i, j),)
 
-        BQ, BH = 2, 4
+        def warm(count, h):
+            if "warm" not in t:
+                t["warm"] = next_bank()
+            cols = slice(h * W // 2, h * W // 2 + P)
+            lhs = (t["inv_a_codes", 1][:, cols].bitcast(FP8X4), t["inv_a_scales", 1][:, cols])
+            rhs = (t["inv_a_codes", 0][:].bitcast(FP8X4), t["inv_a_scales", 0][:])
+            for s in range(count):
+                passes(t["warm"], [(lhs, rhs)])
+
+        BH = 4
         load_vector("mean", mean)
         load_vector("filt", filt)
         make_identity(nc, ident[:])
         clear_plane("inv_b_plane", 2, 0, R)
-        for q in range(2):
-            clear_plane("basis_plane", 3, q, BH * W)
+        clear_plane("basis_plane", 3, 0, BH * W)
+        clear_plane("basis_plane", 3, 1, BH * W)
+        load_plane("inv_b_plane", inv_b_scales, 0, R, nc.gpsimd)
+        load_plane("basis_plane", basis_scales, 0, BH * W, nc.gpsimd)
         load_inv_a(0)
         load_a(0)
         load_b(0)
         load_inv_a(1)
         load_inv_a(2)
-        load_plane("inv_b_plane", inv_b_scales, 0, R)
         load_words("inv_b", inv_b_words, 0, 1)
         load_b(1)
         load_words("inv_b", inv_b_words, 1, 2)
-        load_plane("basis_plane", basis_scales, 0, BH * W)
-        load_words("basis", basis_words, 0, 2)
-        load_words("basis", basis_words, 2, 2)
+        load_words("basis", basis_words, 0, 4)
         load_b(2)
         load_a(1)
-        load_plane("basis_plane", basis_scales, 1, BH * W)
-        load_words("basis", basis_words, 4, 2)
-        load_words("basis", basis_words, 6, 2)
+        load_plane("basis_plane", basis_scales, 1, BH * W, nc.sync)
+        load_words("basis", basis_words, 4, 4)
         load_b(3)
 
         for j in range(3):
@@ -322,18 +329,18 @@ def tile_filtered_deim_advection_s3_kernel(
         turn(fb(0))
         spread_copy(2)
         gather(fa(0) + fa(1))
-        gather(fb(0))
         quantise(fa(0) + fa(1))
         coeff_a(0, 0)
         coeff_a(1, 0)
         weave_inv_a(1, 0, False)
         weave_inv_a(1, 1, True)
-        quantise(fb(0))
+        gather(fb(0))
         quantise_inv_a(1, 0)
-        weave_inv_a(2, 0, False)
-        weave_inv_a(2, 1, True)
         quantise_inv_a(1, 1)
         coeff_a(0, 1)
+        weave_inv_a(2, 0, False)
+        weave_inv_a(2, 1, True)
+        quantise(fb(0))
         coeff_b(0, 0)
         quantise_inv_a(2, 0)
         quantise_inv_a(2, 1)
@@ -359,45 +366,51 @@ def tile_filtered_deim_advection_s3_kernel(
         gather(c2(0))
         coeff(1, 2)
         offset(1, 0)
+        offset(1, 1)
         quantise(c01(0))
         quantise(c2(0))
-        offset(1, 1)
         damp(1, 0)
         offset(1, 2)
         damp(1, 1)
         damp(1, 2)
         for n in range(3):
             expand(0, n)
-        turn_round([c01(1), c2(1)])
+        turn(c01(1))
+        turn(c2(1))
         product("b", 2)
         product("a", 2)
+        gather(c01(1), True)
+        gather(c2(1))
         product("a", 3)
+        quantise(c01(1))
+        quantise(c2(1))
         expand(0, 3)
-        for n in range(0, 2):
-            expand(1, n)
-        turn_round([fb(2), fa(2) + fa(3)])
-        for n in range(2, 4):
+        turn(fb(2))
+        turn(fa(2) + fa(3))
+        gather(fb(2))
+        gather(fa(2) + fa(3), True)
+        quantise(fa(2) + fa(3))
+        quantise(fb(2))
+        for n in range(0, 3):
             expand(1, n)
         for j in range(3):
             coeff(2, j)
         filter_tile(2)
         product("b", 3)
-        for n in range(4, 6):
+        expand(1, 3)
+        for n in range(4, 8):
             expand(0, n)
-        for n in range(4, 6):
-            expand(1, n)
-        for n in range(6, 8):
-            expand(0, n)
-        turn_round([c01(2), c2(2), fb(3)])
-        for n in range(6, 8):
+        expand(1, 4)
+        turn_round([fb(3), c01(2), c2(2)])
+        for n in range(5, 8):
             expand(1, n)
         for j in range(3):
             coeff(3, j)
         filter_tile(3)
-        for n in range(0, 6):
+        for n in range(0, 5):
             expand(2, n)
         turn_round([c01(3), c2(3)])
-        for n in range(6, 8):
+        for n in range(5, 8):
             expand(2, n)
         for n in range(8):
-            expand(3, n, on_vector=(n % 2 == 1), alone=(n >= 2))
+            expand(3, n, on_vector=(n % 2 == 1), alone=(n >= 4))

@@ -50,8 +50,14 @@ def tile_filtered_deim_advection_s3_kernel(
                 t[key, i] = tile[:]
 
         def load_a(h):
-            for key, src in (("vel_a", vel_a), ("grad_a", grad_a)):
-                tile = sb.tile([P, 2, KA], BF16, name="%s%d" % (key, h))
+            load_pair(h, (("vel_a", vel_a), ("grad_a", grad_a)))
+
+        def load_bb(h):
+            load_pair(h, (("vel_b", vel_b), ("grad_b", grad_b)))
+
+        def load_pair(h, sources):
+            for key, src in sources:
+                tile = sb.tile([P, 2, src.shape[1]], BF16, name="%s%d" % (key, h))
                 nc.sync.dma_start(out=tile[:], in_=tile_rows(src)[h])
                 for e in range(2):
                     t[key, 2 * h + e] = tile[:, e, :]
@@ -83,24 +89,27 @@ def tile_filtered_deim_advection_s3_kernel(
                 )
 
         def load_vector(key, vec):
-            tile = sb.tile([P, 3, 4], BF16, name=key + "_col")
-            nc.scalar.dma_start(out=tile[:], in_=vec.rearrange("(g w t) -> w g t", g=3, t=4))
+            tile = sb.tile([P, 12], BF16, name=key + "_col")
+            nc.scalar.dma_start(out=tile[:], in_=vec.rearrange("(w c) -> w c", c=12))
             t[key, "col"] = tile
+            t[key, "rows"] = sb.tile([P, 2, 3 * P], F32, name=key + "_rows")
 
-        def spread_turn(j):
+        def spread_turn(key, u):
             bank = next_bank()
-            for c, (key, u) in enumerate([("mean", 0), ("mean", 1), ("filt", 0), ("filt", 1)]):
-                col = t[key, "col"][:].bitcast(F32)[:, j, u : u + 1]
-                nc.tensor.transpose(bank[:, c * P : (c + 1) * P], col.to_broadcast([P, P]), ident[:])
-            t["spread_bank", j] = bank
+            for h in range(3):
+                col = t[key, "col"][:].bitcast(F32)[:, 2 * h + u : 2 * h + u + 1]
+                nc.tensor.transpose(bank[:, h * P : (h + 1) * P], col.to_broadcast([P, P]), ident[:])
+            t["spread_bank", key, u] = bank
 
-        def spread_copy(j, on_vector=False):
-            rows = sb.tile([P, W], F32, name="spread%d" % j)
-            if on_vector:
-                nc.vector.tensor_copy(out=rows[:], in_=t["spread_bank", j][:])
-            else:
-                nc.scalar.copy(out=rows[:], in_=t["spread_bank", j][:])
-            t["spread", j] = rows
+        def spread_copy(key, u, on_vector=False):
+            move = nc.vector.tensor_copy if on_vector else nc.scalar.copy
+            move(
+                out=t[key, "rows"][:, u, :].rearrange("p (w h) -> p w h", h=3),
+                in_=t["spread_bank", key, u][:, : 3 * P].rearrange("p (h w) -> p w h", h=3),
+            )
+
+        def spread(key, j):
+            return t[key, "rows"][:, :, j * P : (j + 1) * P].bitcast(BF16)
 
         def product(part, i):
             vel, grad = t["vel_" + part, i], t["grad_" + part, i]
@@ -190,19 +199,22 @@ def tile_filtered_deim_advection_s3_kernel(
 
         def offset(i, j):
             tile = sb.tile([P, W], F32, name="shifted%d_%d" % (i, j), tag="shifted", bufs=3)
-            mean_rows = t["spread", j][:].bitcast(BF16)[:, :W]
             nc.vector.tensor_tensor(
                 out=tile[:].rearrange("p (u w e) -> p u w e", u=2, e=2),
                 in0=t["c_bank", i, j][:].rearrange("p (w u e) -> p u w e", u=2, e=2),
-                in1=mean_rows.rearrange("p (u w e) -> p u w e", u=2, e=2),
+                in1=spread("mean", j).rearrange("p u (w e) -> p u w e", e=2),
                 op=ADD,
             )
             t["shifted", i, j] = tile
 
         def damp(i, j):
             tile = sb.tile([P, W], BF16, name="c%d_%d" % (i, j), tag="c", bufs=4)
-            filt_rows = t["spread", j][:].bitcast(BF16)[:, W:]
-            nc.vector.tensor_tensor(out=tile[:], in0=t["shifted", i, j][:], in1=filt_rows, op=MULT)
+            nc.vector.tensor_tensor(
+                out=tile[:].rearrange("p (u c) -> p u c", u=2),
+                in0=t["shifted", i, j][:].rearrange("p (u c) -> p u c", u=2),
+                in1=spread("filt", j),
+                op=MULT,
+            )
             words = tile[:].bitcast(F32)
             t["words", "c", i, j] = [words[:, u * P : (u + 1) * P] for u in range(2)]
 
@@ -314,10 +326,11 @@ def tile_filtered_deim_advection_s3_kernel(
         load_words("basis", basis_words, 4, 4)
         load_b(3)
 
-        for j in range(3):
-            spread_turn(j)
-        spread_copy(0)
-        spread_copy(1, True)
+        for key in ("mean", "filt"):
+            for u in range(2):
+                spread_turn(key, u)
+        spread_copy("mean", 0)
+        spread_copy("mean", 1, True)
         weave_inv_a(0, 0, False)
         weave_inv_a(0, 1, True)
         product("a", 0)
@@ -327,7 +340,8 @@ def tile_filtered_deim_advection_s3_kernel(
         quantise_inv_a(0, 1)
         product("b", 0)
         turn(fb(0))
-        spread_copy(2)
+        spread_copy("filt", 0)
+        spread_copy("filt", 1)
         gather(fa(0) + fa(1))
         quantise(fa(0) + fa(1))
         coeff_a(0, 0)
@@ -351,24 +365,28 @@ def tile_filtered_deim_advection_s3_kernel(
         turn(fb(1))
         coeff_b(0, 1)
         coeff_b(0, 2)
+        coeff_a(1, 2)
         gather(fb(1))
         damp(0, 0)
+        turn(c1(0, 0))
+        gather(c1(0, 0))
         offset(0, 1)
         quantise(fb(1))
         coeff_b(1, 0)
         coeff_b(1, 1)
         offset(0, 2)
         damp(0, 1)
+        turn(c1(0, 1))
+        gather(c1(0, 1))
         damp(0, 2)
-        turn(c01(0))
-        turn(c2(0))
-        gather(c01(0))
-        gather(c2(0))
-        coeff(1, 2)
+        turn(c1(0, 2))
+        gather(c1(0, 2))
+        coeff_b(1, 2)
+        quantise(c1(0, 0))
         offset(1, 0)
+        quantise(c1(0, 1))
+        quantise(c1(0, 2))
         offset(1, 1)
-        quantise(c01(0))
-        quantise(c2(0))
         damp(1, 0)
         offset(1, 2)
         damp(1, 1)

from contextlib import ExitStack

import concourse.mybir as mybir
from concourse.masks import make_identity

M, KA, KB, R, N = 512, 512, 1024, 1536, 4096
FLOPS = 2 * M * (KA + KB) * R + 2 * M * R * N

F32 = mybir.dt.float32
BF16 = mybir.dt.bfloat16
I32 = mybir.dt.int32
U32 = mybir.dt.uint32
U8 = mybir.dt.uint8
FP8X4 = mybir.dt.float8_e4m3fn_x4
FP4X4 = mybir.dt.float4_e2m1fn_x4
ADD = mybir.AluOpType.add
MULT = mybir.AluOpType.mult

P = 128
W = 512
BANKS = 8


def tile_filtered_deim_advection_s3_kernel(
    tc, vel_a, grad_a, vel_b, grad_b, inv_a, inv_b_words, inv_b_scales, mean, filt, basis_words, basis_scales, out
):
    nc = tc.nc
    with ExitStack() as ctx:
        sb = ctx.enter_context(tc.tile_pool(name="sb", bufs=1))
        ps = ctx.enter_context(tc.psum_pool(name="ps", bufs=1))
        ctx.enter_context(tc.manual_schedule())

        taken = []

        def next_bank():
            k = len(taken)
            bank = ps.tile([P, W], F32, name="bank%d" % k, tag="bank%d" % (k % BANKS))
            taken.append(bank)
            return bank

        t = {}

        def tile_rows(dram):
            return dram.rearrange("(h p e) c -> h p e c", p=P, e=2)

        def load_b(i):
            for key, src in (("vel_b", vel_b), ("grad_b", grad_b)):
                tile = sb.tile([P, KB], BF16, name="%s%d" % (key, i))
                nc.sync.dma_start(out=tile[:], in_=tile_rows(src)[i // 2][:, i % 2, :])
                t[key, i] = tile[:]

        def load_a(h):
            load_pair(h, (("vel_a", vel_a), ("grad_a", grad_a)))

        def load_bb(h):
            load_pair(h, (("vel_b", vel_b), ("grad_b", grad_b)))

        def load_pair(h, sources):
            for key, src in sources:
                tile = sb.tile([P, 2, src.shape[1]], BF16, name="%s%d" % (key, h))
                nc.sync.dma_start(out=tile[:], in_=tile_rows(src)[h])
                for e in range(2):
                    t[key, 2 * h + e] = tile[:, e, :]

        def load_inv_a(j):
            tile = sb.tile([P, 4, W], BF16, name="inv_a_raw%d" % j)
            nc.sync.dma_start(out=tile[:], in_=inv_a[:, j * W : (j + 1) * W].rearrange("(p t) c -> p t c", t=4))
            t["inv_a_raw", j] = tile

        def load_words(key, src, first, count):
            groups = src.shape[0]
            tile = sb.tile([P, groups, 2 * W * count], U8, name="%s%d" % (key, first), align_bytes=64)
            words = src.bitcast(I32).rearrange("g p w -> p g w")
            nc.sync.dma_start(out=tile[:].bitcast(I32), in_=words[:, :, first * W // 2 : (first + count) * W // 2])
            for s in range(count):
                t[key, first + s] = tile[:, :, s * 2 * W : (s + 1) * 2 * W]

        def clear_plane(key, groups, j, cols):
            tile = sb.tile([P, groups, cols], U8, name="%s%d" % (key, j), align_bytes=64)
            nc.vector.memset(tile[:].bitcast(I32), 0)
            t[key, j] = tile

        def load_plane(key, src, j, cols, queue):
            rows = src.bitcast(I32).rearrange("g (q r) w -> r q g w", r=4)
            for r in range(4):
                queue.dma_start(
                    out=t[key, j][:].bitcast(I32)[r:P:32, :, :],
                    in_=rows[r][:, :, j * cols // 4 : (j + 1) * cols // 4],
                )

        def load_vector(key, vec):
            tile = sb.tile([P, 12], BF16, name=key + "_col")
            nc.scalar.dma_start(out=tile[:], in_=vec.rearrange("(w c) -> w c", c=12))
            t[key, "col"] = tile
            t[key, "rows"] = sb.tile([P, 2, 3 * P], F32, name=key + "_rows")

        def spread_turn(key, u):
            bank = next_bank()
            for h in range(3):
                col = t[key, "col"][:].bitcast(F32)[:, 2 * h + u : 2 * h + u + 1]
                nc.tensor.transpose(bank[:, h * P : (h + 1) * P], col.to_broadcast([P, P]), ident[:])
            t["spread_bank", key, u] = bank

        def spread_copy(key, u, on_vector=False):
            move = nc.vector.tensor_copy if on_vector else nc.scalar.copy
            move(
                out=t[key, "rows"][:, u, :].rearrange("p (w h) -> p w h", h=3),
                in_=t["spread_bank", key, u][:, : 3 * P].rearrange("p (h w) -> p w h", h=3),
            )

        def spread(key, j):
            return t[key, "rows"][:, :, j * P : (j + 1) * P].bitcast(BF16)

        def product(part, i):
            vel, grad = t["vel_" + part, i], t["grad_" + part, i]
            width = vel.shape[1]
            tile = sb.tile([P, width], BF16, name="f%s%d" % (part, i), tag="f" + part, bufs=2)
            nc.vector.tensor_tensor(
                out=tile[:].rearrange("p (u w e) -> p u w e", u=2, e=2),
                in0=vel.rearrange("p (w u e) -> p u w e", u=2, e=2),
                in1=grad.rearrange("p (w u e) -> p u w e", u=2, e=2),
                op=MULT,
            )
            words = tile[:].bitcast(F32)
            half = width // 4
            for g in range(width // W):
                t["words", "f" + part, i, g] = [words[:, u * half + g * P : u * half + (g + 1) * P] for u in range(2)]

        def turn(keys):
            bank = next_bank()
            for s, key in enumerate(keys):
                for u in range(2):
                    c = 2 * s + u
                    nc.tensor.transpose(bank[:, c * P : (c + 1) * P], t[("words",) + key][u], ident[:])
            t["turned", keys] = bank

        def gather(keys, on_vector=False):
            n = len(keys)
            move = nc.vector.tensor_copy if on_vector else nc.scalar.copy
            tile = sb.tile([P, 2 * W], BF16, name="grouped_%s%d_%d" % keys[0], tag="grouped", bufs=4, align_bytes=64)
            move(
                out=tile[:, : n * W].bitcast(F32).rearrange("p (s m u) -> p s m u", s=n, u=2),
                in_=t["turned", keys][:, : n * 2 * P].rearrange("p (s u m) -> p s m u", s=n, u=2),
            )
            t["grouped", keys] = tile

        def quantise(keys):
            n = len(keys)
            codes = sb.tile([P, n * P], U32, name="codes_%s%d_%d" % keys[0], align_bytes=64)
            scales = sb.tile([P, n * P], U8, name="scales_%s%d_%d" % keys[0], align_bytes=64)
            nc.vector.quantize_mx(out=codes[:].bitcast(FP8X4), scales=scales[:], in_=t["grouped", keys][:, : n * W])
            for s, key in enumerate(keys):
                t[("lhs",) + key] = (codes[:, s * P : (s + 1) * P].bitcast(FP8X4), scales[:, s * P : (s + 1) * P])

        def weave_inv_a(j, h, on_scalar):
            tile = sb.tile([P, W // 2, 4], BF16, name="inv_a_woven%d_%d" % (j, h), align_bytes=64)
            src = t["inv_a_raw", j][:, :, h * W // 2 : (h + 1) * W // 2].rearrange("p t (c i) -> p c t i", i=4)
            dst = tile[:].rearrange("p (c i) t -> p c t i", i=4)
            if on_scalar:
                nc.scalar.copy(out=dst, in_=src)
            else:
                nc.vector.tensor_copy(out=dst, in_=src)
            t["inv_a_woven", j, h] = tile

        def quantise_inv_a(j, h):
            if h == 0:
                t["inv_a_codes", j] = sb.tile([P, W], U32, name="inv_a_codes%d" % j, align_bytes=64)
                t["inv_a_scales", j] = sb.tile([P, W], U8, name="inv_a_scales%d" % j, align_bytes=64)
            cols = slice(h * W // 2, (h + 1) * W // 2)
            nc.vector.quantize_mx(
                out=t["inv_a_codes", j][:, cols].bitcast(FP8X4),
                scales=t["inv_a_scales", j][:, cols],
                in_=t["inv_a_woven", j, h][:].rearrange("p c t -> p (c t)"),
            )

        def passes(bank, pairs, first=True, last=True):
            for s, (lhs, rhs) in enumerate(pairs):
                nc.tensor.matmul_mx(
                    out=bank[:], lhsT=lhs[0], lhsT_scale=lhs[1], rhs=rhs[0], rhs_scale=rhs[1],
                    start=(first and s == 0), stop=(last and s == len(pairs) - 1),
                )

        def coeff_b(i, j):
            bank = t["c_bank", i, j]
            pairs = []
            for g in range(2):
                rhs = (t["inv_b", j][:, g, :].bitcast(FP4X4), t["inv_b_plane", 0][:, g, j * W : (j + 1) * W])
                pairs.append((t["lhs", "fb", i, g], rhs))
            passes(bank, pairs, first=False)

        def coeff_a(i, j):
            t["c_bank", i, j] = next_bank()
            rhs = (t["inv_a_codes", j][:].bitcast(FP8X4), t["inv_a_scales", j][:])
            passes(t["c_bank", i, j], [(t["lhs", "fa", i, 0], rhs)], last=False)

        def coeff(i, j):
            coeff_a(i, j)
            coeff_b(i, j)

        def offset(i, j):
            tile = sb.tile([P, W], F32, name="shifted%d_%d" % (i, j), tag="shifted", bufs=3)
            nc.vector.tensor_tensor(
                out=tile[:].rearrange("p (u w e) -> p u w e", u=2, e=2),
                in0=t["c_bank", i, j][:].rearrange("p (w u e) -> p u w e", u=2, e=2),
                in1=spread("mean", j).rearrange("p u (w e) -> p u w e", e=2),
                op=ADD,
            )
            t["shifted", i, j] = tile

        def damp(i, j):
            tile = sb.tile([P, W], BF16, name="c%d_%d" % (i, j), tag="c", bufs=4)
            nc.vector.tensor_tensor(
                out=tile[:].rearrange("p (u c) -> p u c", u=2),
                in0=t["shifted", i, j][:].rearrange("p (u c) -> p u c", u=2),
                in1=spread("filt", j),
                op=MULT,
            )
            words = tile[:].bitcast(F32)
            t["words", "c", i, j] = [words[:, u * P : (u + 1) * P] for u in range(2)]

        def expand(i, n, on_vector=False, alone=False):
            bank = next_bank()
            pairs = []
            for g in range(3):
                words = t["basis", n][:, g, :].bitcast(FP4X4)
                plane = t["basis_plane", n // BH][:, g, (n % BH) * W : (n % BH + 1) * W]
                pairs.append((t["lhs", "c", i, g], (words, plane)))
            passes(bank, pairs)
            if n % 2 == 0:
                t["res", i, n // 2] = sb.tile([P, 2 * W], F32, name="res%d_%d" % (i, n // 2))
            res = t["res", i, n // 2]
            cols = slice((n % 2) * W, (n % 2 + 1) * W)
            if on_vector:
                nc.vector.tensor_copy(out=res[:, cols], in_=bank[:])
            else:
                nc.scalar.copy(out=res[:, cols], in_=bank[:])
            rows = tile_rows(out)[i // 2][:, i % 2, :]
            if alone:
                nc.sync.dma_start(out=rows[:, n * W : (n + 1) * W], in_=res[:, cols])
            elif n % 2 == 1:
                nc.sync.dma_start(out=rows[:, (n - 1) * W : (n + 1) * W], in_=res[:])

        ident = sb.tile([P, P], F32, name="ident")

        def fb(i):
            return (("fb", i, 0), ("fb", i, 1))

        def fa(i):
            return (("fa", i, 0),)

        def c01(i):
            return (("c", i, 0), ("c", i, 1))

        def c2(i):
            return (("c", i, 2),)

        def filter_tile(i):
            offset(i, 0)
            offset(i, 1)
            damp(i, 0)
            offset(i, 2)
            damp(i, 1)
            damp(i, 2)

        def turn_round(sets):
            for s in sets:
                turn(s)
            gather(sets[0], True)
            for s in sets[1:]:
                gather(s)
            for s in sets:
                quantise(s)


        def expand_last(i, n):
            rows = tile_rows(out)[i // 2][:, i % 2, :]
            res = t["res", i, n // 2]
            for s in range(4):
                bank = next_bank()
                pairs = []
                for g in range(3):
                    words = t["basis", n][:, g, s * 2 * P : (s + 1) * 2 * P].bitcast(FP4X4)
                    plane = t["basis_plane", n // BH][:, g, (n % BH) * W + s * P : (n % BH) * W + (s + 1) * P]
                    pairs.append((t["lhs", "c", i, g], (words, plane)))
                passes(bank[:, :P], pairs)
                cols = slice(W + s * P, W + (s + 1) * P)
                if s % 2 == 1:
                    nc.vector.tensor_copy(out=res[:, cols], in_=bank[:, :P])
                    nc.sync.dma_start(out=rows[:, n * W + (s - 1) * P : n * W + (s + 1) * P], in_=res[:, W + (s - 1) * P : W + (s + 1) * P])
                else:
                    nc.scalar.copy(out=res[:, cols], in_=bank[:, :P])

        def c1(i, j):
            return (("c", i, j),)

        def warm(count, h):
            if "warm" not in t:
                t["warm"] = next_bank()
            cols = slice(h * W // 2, h * W // 2 + P)
            lhs = (t["inv_a_codes", 1][:, cols].bitcast(FP8X4), t["inv_a_scales", 1][:, cols])
            rhs = (t["inv_a_codes", 0][:].bitcast(FP8X4), t["inv_a_scales", 0][:])
            for s in range(count):
                passes(t["warm"], [(lhs, rhs)])

        BH = 4
        load_vector("mean", mean)
        load_vector("filt", filt)
        make_identity(nc, ident[:])
        clear_plane("inv_b_plane", 2, 0, R)
        clear_plane("basis_plane", 3, 0, BH * W)
        clear_plane("basis_plane", 3, 1, BH * W)
        load_plane("inv_b_plane", inv_b_scales, 0, R, nc.gpsimd)
        load_plane("basis_plane", basis_scales, 0, BH * W, nc.gpsimd)
        load_inv_a(0)
        load_a(0)
        load_b(0)
        load_inv_a(1)
        load_inv_a(2)
        load_words("inv_b", inv_b_words, 0, 1)
        load_b(1)
        load_words("inv_b", inv_b_words, 1, 2)
        load_words("basis", basis_words, 0, 4)
        load_b(2)
        load_a(1)
        load_plane("basis_plane", basis_scales, 1, BH * W, nc.sync)
        load_words("basis", basis_words, 4, 4)
        load_b(3)

        for key in ("mean", "filt"):
            for u in range(2):
                spread_turn(key, u)
        spread_copy("mean", 0)
        spread_copy("mean", 1, True)
        weave_inv_a(0, 0, False)
        weave_inv_a(0, 1, True)
        product("a", 0)
        product("a", 1)
        turn(fa(0) + fa(1))
        quantise_inv_a(0, 0)
        quantise_inv_a(0, 1)
        product("b", 0)
        turn(fb(0))
        spread_copy("filt", 0)
        spread_copy("filt", 1)
        gather(fa(0) + fa(1))
        quantise(fa(0) + fa(1))
        coeff_a(0, 0)
        coeff_a(1, 0)
        weave_inv_a(1, 0, False)
        weave_inv_a(1, 1, True)
        gather(fb(0))
        quantise_inv_a(1, 0)
        quantise_inv_a(1, 1)
        coeff_a(0, 1)
        weave_inv_a(2, 0, False)
        weave_inv_a(2, 1, True)
        quantise(fb(0))
        coeff_b(0, 0)
        quantise_inv_a(2, 0)
        quantise_inv_a(2, 1)
        coeff_a(0, 2)
        coeff_a(1, 1)
        product("b", 1)
        offset(0, 0)
        turn(fb(1))
        coeff_b(0, 1)
        coeff_b(0, 2)
        coeff_a(1, 2)
        gather(fb(1))
        damp(0, 0)
        turn(c1(0, 0))
        gather(c1(0, 0))
        offset(0, 1)
        quantise(fb(1))
        coeff_b(1, 0)
        coeff_b(1, 1)
        offset(0, 2)
        damp(0, 1)
        turn(c1(0, 1))
        gather(c1(0, 1))
        damp(0, 2)
        turn(c1(0, 2))
        gather(c1(0, 2))
        coeff_b(1, 2)
        quantise(c1(0, 0))
        offset(1, 0)
        quantise(c1(0, 1))
        quantise(c1(0, 2))
        offset(1, 1)
        damp(1, 0)
        offset(1, 2)
        damp(1, 1)
        damp(1, 2)
        for n in range(3):
            expand(0, n)
        turn(c01(1))
        turn(c2(1))
        product("b", 2)
        product("a", 2)
        gather(c01(1), True)
        gather(c2(1))
        product("a", 3)
        quantise(c01(1))
        quantise(c2(1))
        expand(0, 3)
        turn(fb(2))
        turn(fa(2) + fa(3))
        gather(fb(2))
        gather(fa(2) + fa(3), True)
        quantise(fa(2) + fa(3))
        quantise(fb(2))
        for n in range(0, 3):
            expand(1, n)
        for j in range(3):
            coeff(2, j)
        filter_tile(2)
        product("b", 3)
        expand(1, 3)
        for n in range(4, 8):
            expand(0, n)
        expand(1, 4)
        turn_round([fb(3), c01(2), c2(2)])
        for n in range(5, 8):
            expand(1, n)
        for j in range(3):
            coeff(3, j)
        filter_tile(3)
        for n in range(0, 5):
            expand(2, n)
        turn_round([c01(3), c2(3)])
        for n in range(5, 8):
            expand(2, n)
        for n in range(8):
            expand(3, n, on_vector=(n % 2 == 1), alone=(n >= 4))
